import numpy as np
import ml_dtypes


def mxq(x, axis, fmt="e4m3"):
    dtype, down = {"e4m3": (ml_dtypes.float8_e4m3fn, 7), "e5m2": (ml_dtypes.float8_e5m2, 14)}[fmt]
    v = np.moveaxis(np.asarray(x, np.float32).astype(ml_dtypes.bfloat16).astype(np.float64), axis, -1)
    blocks = v.reshape(v.shape[:-1] + (-1, 32))
    amax = np.abs(blocks).max(-1, keepdims=True)
    byte = np.maximum(np.where(amax > 0, np.frexp(amax)[1] - 1 + 127, 0) - down, 1)
    scale = np.exp2(byte - 127.0)
    codes = (blocks / scale).astype(np.float32).astype(dtype).astype(np.float64)
    return np.moveaxis((codes * scale).reshape(v.shape), -1, axis)


WIDE = False


def mx_kscale(k):
    if not WIDE:
        return np.ones(k)
    levels = np.array([10, -10, 5, -5, 0])
    if k % 512:
        return np.exp2(np.random.permutation(np.resize(levels, k // 32))).repeat(32)
    a = np.empty((k // 512, 16))
    for p in range(k // 512):
        a[p, :8] = np.random.permutation(np.resize(levels, 8))
        for g in range(8):
            far = levels[np.abs(levels - a[p, g]) >= 10]
            a[p, g + 8] = far[np.random.randint(len(far))]
    return np.exp2(a.ravel()).repeat(32)


def f64(x):
    return np.asarray(x).astype(np.float64)


def striped8(idx):
    return np.asarray(idx).reshape(8, -1, 16).transpose(0, 2, 1).reshape(128, -1).astype(np.uint16)


def unstriped8(offs):
    return offs.reshape(8, 16, -1).transpose(0, 2, 1).reshape(8, -1).astype(np.int64)


def pick8(x, idx, run):
    r = np.arange(len(x))
    return x[r[:, None], idx[r % (8 * run) // run]]


E2M1 = np.array([0.0, 0.5, 1.0, 1.5, 2.0, 3.0, 4.0, 6.0, -0.0, -0.5, -1.0, -1.5, -2.0, -3.0, -4.0, -6.0])


def pack_weight(w, fmt):
    k, n = w.shape
    w = f64(np.asarray(w, np.float32).astype(ml_dtypes.bfloat16)).reshape(k // 32, 32, n)
    amax = np.abs(w).max(1)
    if fmt == "e4m3":
        byte = np.frexp(amax)[1] - 1 + 127 - 7
    else:
        mant, ex = np.frexp(amax / 6.0)
        byte = np.where(mant > 0.5, ex, ex - 1) + 127
    byte = np.clip(np.where(amax > 0, byte, 1), 1, 254)
    scaled = (w * np.exp2(127.0 - byte)[:, None, :]).reshape(k, n).astype(np.float32)
    by_word = np.ascontiguousarray(scaled.reshape(k // 512, 128, 4, n).transpose(0, 1, 3, 2))
    if fmt == "e4m3":
        words = by_word.astype(ml_dtypes.float8_e4m3fn).view(np.uint8)
    else:
        c = by_word.astype(ml_dtypes.float4_e2m1fn).view(np.uint8) & 0xF
        words = (c[..., 0::2] | (c[..., 1::2] << 4)).reshape(k // 512, 128, 2 * n)
    return np.ascontiguousarray(words), np.ascontiguousarray(byte.astype(np.uint8).reshape(k // 512, 16, n))


def unpack_weight(words, scales, fmt):
    g, _, n = scales.shape
    words = np.ascontiguousarray(words).reshape(g, 128, n, -1)
    if fmt == "e4m3":
        vals = words.view(ml_dtypes.float8_e4m3fn).astype(np.float64)
    else:
        nib = np.empty((g, 128, n, 4), np.uint8)
        nib[..., 0::2] = words & 0xF
        nib[..., 1::2] = words >> 4
        vals = E2M1[nib]
    vals = vals * np.repeat(np.exp2(scales.astype(np.float64) - 127.0), 8, axis=1)[..., None]
    return vals.transpose(0, 1, 3, 2).reshape(g * 512, n)


def sigmoid(v):
    return 1.0 / (1.0 + np.exp(-v))


D, T, I, Q = 512, 1024, 512, 128


def setup_inputs():
    n = np.random.standard_normal
    idx = np.stack([np.random.permutation(T)[:I] for _ in range(8)])
    idx2 = np.stack([np.random.permutation(T)[:I] for _ in range(8)])
    idx3 = np.stack([np.random.permutation(T)[:I] for _ in range(8)])
    idx4 = np.stack([np.random.permutation(T)[:I] for _ in range(8)])
    fd = mx_kscale(D)
    keysp = pack_weight(n((D, T)) / fd[:, None], "e4m3")
    return {
        "query": (n((D, Q)) * 1.2 / np.sqrt(D) * fd[:, None]).astype(np.float32),
        "keys_words": keysp[0],
        "keys_scales": keysp[1],
        "lam": (np.random.uniform(0.5, 1.5, (Q, 1))).astype(np.float32),
        "old": (1.0 * n((Q, T))).astype(np.float32),
        "offs": striped8(idx),
        "offs2": striped8(idx2),
        "offs3": striped8(idx3),
        "offs4": striped8(idx4),
    }


def reference(query, keys_words, keys_scales, lam, old, offs, offs2, offs3, offs4):
    idx = unstriped8(offs)
    idx2 = unstriped8(offs2)
    idx3 = unstriped8(offs3)
    idx4 = unstriped8(offs4)
    keysu = unpack_weight(keys_words, keys_scales, "e4m3")
    queryq = mxq(f64(query), 0, "e4m3")
    a = queryq.T @ keysu
    g1 = sigmoid(pick8(a, idx2, 16) * 2.0)
    w = (pick8(a, idx, 16) * g1 + pick8(a, idx3, 16) * (1.0 - g1)) * f64(lam)
    f1 = np.zeros((Q, T))
    f1[np.arange(Q)[:, None], idx4[np.arange(Q) % 128 // 16]] = w
    y = f64(old) + f1
    return y

@@ -1,0 +1,137 @@
+from contextlib import ExitStack
+
+import concourse.mybir as mybir
+
+D, T, I, Q = 512, 1024, 512, 128
+FLOPS = 2 * D * T * Q
+
+F32 = mybir.dt.float32
+BF16 = mybir.dt.bfloat16
+I32 = mybir.dt.int32
+U32 = mybir.dt.uint32
+U16 = mybir.dt.uint16
+U8 = mybir.dt.uint8
+FP8X4 = mybir.dt.float8_e4m3fn_x4
+ALU = mybir.AluOpType
+ACT = mybir.ActivationFunctionType
+
+P = 128
+PACK = 4
+GROUP = 16
+HALF = I // 2
+KEY_LOADS = 2
+SCORE_COLS = (256, 256, 256, 128, 128)
+STORE_COLS = (128, 256, 384, 256)
+
+
+def tile_attend_conditioned_lean_putold_heads_kernel(
+    tc, query, keys_words, keys_scales, lam, old, offs, offs2, offs3, offs4, out
+):
+    nc = tc.nc
+    with ExitStack() as ctx:
+        lists = ctx.enter_context(tc.tile_pool(name="lists", bufs=1))
+        sb = ctx.enter_context(tc.tile_pool(name="sb", bufs=1))
+        psum = ctx.enter_context(tc.psum_pool(name="psum", bufs=1))
+
+        key_scales = sb.tile([P, T], U8, align_bytes=64)
+        nc.vector.memset(key_scales[:].bitcast(I32), 0)
+
+        q_raw = sb.tile([P, PACK, Q], F32, tag="staged")
+        nc.sync.dma_start(out=q_raw[:], in_=query.rearrange("(p j) q -> p j q", j=PACK))
+
+        for quad in range(4):
+            nc.scalar.dma_start(
+                out=key_scales[32 * quad : 32 * quad + 4, :].bitcast(I32),
+                in_=keys_scales[0, 4 * quad : 4 * quad + 4, :].bitcast(I32),
+            )
+
+        words_hbm = keys_words[0].rearrange("p c r -> p (c r)").bitcast(I32)
+        width = T // KEY_LOADS
+        key_words = []
+        for u in range(KEY_LOADS):
+            part = sb.tile([P, width], I32, name="key_words%d" % u, align_bytes=64)
+            nc.sync.dma_start(out=part[:], in_=words_hbm[:, u * width : (u + 1) * width])
+            key_words.append(part)
+
+        judge = lists.tile([P, I // GROUP], U16)
+        first = lists.tile([P, I // GROUP], U16)
+        second = lists.tile([P, I // GROUP], U16)
+        places = lists.tile([P, I // GROUP], U16)
+        nc.sync.dma_start(judge[:], offs2)
+        nc.sync.dma_start(first[:], offs)
+        lam_col = sb.tile([P, 1], F32)
+        nc.gpsimd.dma_start(out=lam_col[:], in_=lam)
+        nc.sync.dma_start(second[:], offs3)
+        nc.sync.dma_start(places[:], offs4)
+        totals = sb.tile([P, T], F32, tag="staged")
+        nc.sync.dma_start(out=totals[:], in_=old)
+
+        placed = sb.tile([P, T], F32)
+        nc.vector.memset(placed[:], 0.0)
+
+        q_bf = sb.tile([P, Q, PACK], BF16, align_bytes=64)
+        nc.vector.tensor_copy(
+            out=q_bf[:].rearrange("p (c i) j -> p c j i", i=4),
+            in_=q_raw[:].rearrange("p j (c i) -> p c j i", i=4),
+        )
+        q_words = sb.tile([P, Q], U32, align_bytes=64)
+        q_scales = sb.tile([P, Q], U8, align_bytes=64)
+        nc.vector.quantize_mx(
+            out=q_words[:].bitcast(FP8X4),
+            scales=q_scales[:],
+            in_=q_bf[:].rearrange("p q j -> p (q j)"),
+        )
+
+        scores = sb.tile([P, T], F32)
+        c0 = 0
+        for b, n in enumerate(SCORE_COLS):
+            bank = psum.tile([P, n], F32, name="bank%d" % b)
+            u, lo = divmod(c0, width)
+            nc.tensor.matmul_mx(
+                out=bank[:],
+                lhsT=q_words[:].bitcast(FP8X4),
+                lhsT_scale=q_scales[:],
+                rhs=key_words[u][:, lo : lo + n].bitcast(FP8X4),
+                rhs_scale=key_scales[:, c0 : c0 + n],
+                start=True,
+                stop=True,
+            )
+            if b % 2 == 0:
+                nc.scalar.copy(scores[:, c0 : c0 + n], bank[:])
+            else:
+                nc.vector.tensor_copy(scores[:, c0 : c0 + n], bank[:])
+            c0 = c0 + n
+
+        neg_lam = sb.tile([P, 1], F32)
+        nc.vector.tensor_scalar(neg_lam[:], lam_col[:], -1.0, None, ALU.mult)
+
+        a_first = sb.tile([P, I], F32)
+        nc.vector.tensor_copy(a_first[:], scores[:].indirect(first[:]))
+
+        cols = HALF // GROUP
+        for h in range(2):
+            entries = slice(h * cols, (h + 1) * cols)
+            slots = slice(h * HALF, (h + 1) * HALF)
+            gate = sb.tile([P, HALF], F32, name="gate%d" % h)
+            nc.scalar.activation(gate[:], scores[:].indirect(judge[:, entries]), ACT.Sigmoid, scale=2.0)
+            neg_second = sb.tile([P, HALF], F32, name="neg_second%d" % h)
+            nc.scalar.activation(
+                neg_second[:], scores[:].indirect(second[:, entries]), ACT.Copy, scale=neg_lam[:]
+            )
+            term1 = sb.tile([P, HALF], F32, name="term1_%d" % h)
+            nc.vector.scalar_tensor_tensor(
+                term1[:], a_first[:, slots], lam_col[:], gate[:], ALU.mult, ALU.mult
+            )
+            term2 = sb.tile([P, HALF], F32, name="term2_%d" % h)
+            nc.vector.scalar_tensor_tensor(
+                term2[:], gate[:], 1.0, neg_second[:], ALU.subtract, ALU.mult
+            )
+            nc.vector.tensor_tensor(placed[:].indirect(places[:, entries]), term1[:], term2[:], ALU.add)
+
+        c0 = 0
+        for s, n in enumerate(STORE_COLS):
+            result = sb.tile([P, n], F32, name="result%d" % s)
+            nc.vector.tensor_tensor(result[:], placed[:, c0 : c0 + n], totals[:, c0 : c0 + n], ALU.add)
+            queue = nc.sync if s % 2 == 0 else nc.scalar
+            queue.dma_start(out=out[:, c0 : c0 + n], in_=result[:])
+            c0 = c0 + n

@@ -69,6 +69,11 @@ def tile_attend_conditioned_lean_putold_heads_kernel(
         placed = sb.tile([P, T], F32)
         nc.vector.memset(placed[:], 0.0)
 
+        warm_in = sb.tile([P, 1], F32)
+        warm_out = sb.tile([P, 1], F32)
+        nc.vector.memset(warm_in[:], 0.0)
+        nc.scalar.activation(warm_out[:], warm_in[:], ACT.Sigmoid)
+
         q_bf = sb.tile([P, Q, PACK], BF16, align_bytes=64)
         nc.vector.tensor_copy(
             out=q_bf[:].rearrange("p (c i) j -> p c j i", i=4),

@@ -17,11 +17,14 @@ ACT = mybir.ActivationFunctionType
 
 P = 128
 PACK = 4
-GROUP = 16
-HALF = I // 2
-KEY_LOADS = 2
+QUADRANTS = 4
+SCALE_ROWS = 4
+HEAD_ROWS = 16
+KEY_COLS = T // 2
+SLOT_PARTS = 2
+PART = I // SLOT_PARTS
 SCORE_COLS = (256, 256, 256, 128, 128)
-STORE_COLS = (128, 256, 384, 256)
+STORE_COLS = 256
 
 
 def tile_attend_conditioned_lean_putold_heads_kernel(
@@ -39,25 +42,24 @@ def tile_attend_conditioned_lean_putold_heads_kernel(
         q_raw = sb.tile([P, PACK, Q], F32, tag="staged")
         nc.sync.dma_start(out=q_raw[:], in_=query.rearrange("(p j) q -> p j q", j=PACK))
 
-        for quad in range(4):
-            nc.scalar.dma_start(
-                out=key_scales[32 * quad : 32 * quad + 4, :].bitcast(I32),
-                in_=keys_scales[0, 4 * quad : 4 * quad + 4, :].bitcast(I32),
-            )
-
         words_hbm = keys_words[0].rearrange("p c r -> p (c r)").bitcast(I32)
-        width = T // KEY_LOADS
-        key_words = []
-        for u in range(KEY_LOADS):
-            part = sb.tile([P, width], I32, name="key_words%d" % u, align_bytes=64)
-            nc.sync.dma_start(out=part[:], in_=words_hbm[:, u * width : (u + 1) * width])
-            key_words.append(part)
+        key_words = [
+            sb.tile([P, KEY_COLS], I32, name="key_words%d" % u, align_bytes=64) for u in range(T // KEY_COLS)
+        ]
+        judge = lists.tile([P, I // HEAD_ROWS], U16)
+        first = lists.tile([P, I // HEAD_ROWS], U16)
+        second = lists.tile([P, I // HEAD_ROWS], U16)
+        places = lists.tile([P, I // HEAD_ROWS], U16)
 
-        judge = lists.tile([P, I // GROUP], U16)
-        first = lists.tile([P, I // GROUP], U16)
-        second = lists.tile([P, I // GROUP], U16)
-        places = lists.tile([P, I // GROUP], U16)
+        nc.sync.dma_start(out=key_words[0][:], in_=words_hbm[:, :KEY_COLS])
+        for r in range(QUADRANTS):
+            queue = nc.scalar if r < QUADRANTS // 2 else nc.sync
+            queue.dma_start(
+                out=key_scales[32 * r : 32 * r + SCALE_ROWS, :].bitcast(I32),
+                in_=keys_scales[0, SCALE_ROWS * r : SCALE_ROWS * (r + 1), :].bitcast(I32),
+            )
         nc.sync.dma_start(judge[:], offs2)
+        nc.sync.dma_start(out=key_words[1][:], in_=words_hbm[:, KEY_COLS:])
         nc.sync.dma_start(first[:], offs)
         lam_col = sb.tile([P, 1], F32)
         nc.gpsimd.dma_start(out=lam_col[:], in_=lam)
@@ -88,55 +90,56 @@ def tile_attend_conditioned_lean_putold_heads_kernel(
         )
 
         scores = sb.tile([P, T], F32)
-        c0 = 0
+        t0 = 0
         for b, n in enumerate(SCORE_COLS):
             bank = psum.tile([P, n], F32, name="bank%d" % b)
-            u, lo = divmod(c0, width)
+            u, lo = divmod(t0, KEY_COLS)
             nc.tensor.matmul_mx(
                 out=bank[:],
                 lhsT=q_words[:].bitcast(FP8X4),
                 lhsT_scale=q_scales[:],
                 rhs=key_words[u][:, lo : lo + n].bitcast(FP8X4),
-                rhs_scale=key_scales[:, c0 : c0 + n],
+                rhs_scale=key_scales[:, t0 : t0 + n],
                 start=True,
                 stop=True,
             )
             if b % 2 == 0:
-                nc.scalar.copy(scores[:, c0 : c0 + n], bank[:])
+                nc.scalar.copy(scores[:, t0 : t0 + n], bank[:])
             else:
-                nc.vector.tensor_copy(scores[:, c0 : c0 + n], bank[:])
-            c0 = c0 + n
+                nc.vector.tensor_copy(scores[:, t0 : t0 + n], bank[:])
+            t0 = t0 + n
 
         neg_lam = sb.tile([P, 1], F32)
-        nc.vector.tensor_scalar(neg_lam[:], lam_col[:], -1.0, None, ALU.mult)
+        nc.scalar.activation(neg_lam[:], lam_col[:], ACT.Copy, scale=-1.0)
 
-        a_first = sb.tile([P, I], F32)
-        nc.vector.tensor_copy(a_first[:], scores[:].indirect(first[:]))
+        cols = PART // HEAD_ROWS
+        a_first = []
+        for h in range(SLOT_PARTS):
+            picked = sb.tile([P, PART], F32, name="a_first%d" % h)
+            nc.vector.tensor_copy(picked[:], scores[:].indirect(first[:, h * cols : (h + 1) * cols]))
+            a_first.append(picked)
 
-        cols = HALF // GROUP
-        for h in range(2):
+        for h in range(SLOT_PARTS):
             entries = slice(h * cols, (h + 1) * cols)
-            slots = slice(h * HALF, (h + 1) * HALF)
-            gate = sb.tile([P, HALF], F32, name="gate%d" % h)
+            gate = sb.tile([P, PART], F32, name="gate%d" % h, tag="gate")
             nc.scalar.activation(gate[:], scores[:].indirect(judge[:, entries]), ACT.Sigmoid, scale=2.0)
-            neg_second = sb.tile([P, HALF], F32, name="neg_second%d" % h)
+            neg_second = sb.tile([P, PART], F32, name="neg_second%d" % h)
             nc.scalar.activation(
                 neg_second[:], scores[:].indirect(second[:, entries]), ACT.Copy, scale=neg_lam[:]
             )
-            term1 = sb.tile([P, HALF], F32, name="term1_%d" % h)
+            term1 = sb.tile([P, PART], F32, name="term1_%d" % h)
             nc.vector.scalar_tensor_tensor(
-                term1[:], a_first[:, slots], lam_col[:], gate[:], ALU.mult, ALU.mult
+                term1[:], a_first[h][:], lam_col[:], gate[:], ALU.mult, ALU.mult
             )
-            term2 = sb.tile([P, HALF], F32, name="term2_%d" % h)
+            term2 = sb.tile([P, PART], F32, name="term2_%d" % h)
             nc.vector.scalar_tensor_tensor(
                 term2[:], gate[:], 1.0, neg_second[:], ALU.subtract, ALU.mult
             )
             nc.vector.tensor_tensor(placed[:].indirect(places[:, entries]), term1[:], term2[:], ALU.add)
 
-        c0 = 0
-        for s, n in enumerate(STORE_COLS):
-            result = sb.tile([P, n], F32, name="result%d" % s)
-            nc.vector.tensor_tensor(result[:], placed[:, c0 : c0 + n], totals[:, c0 : c0 + n], ALU.add)
+        for s in range(T // STORE_COLS):
+            tokens = slice(s * STORE_COLS, (s + 1) * STORE_COLS)
+            result = sb.tile([P, STORE_COLS], F32, name="result%d" % s)
+            nc.vector.tensor_tensor(result[:], placed[:, tokens], totals[:, tokens], ALU.add)
             queue = nc.sync if s % 2 == 0 else nc.scalar
-            queue.dma_start(out=out[:, c0 : c0 + n], in_=result[:])
-            c0 = c0 + n
+            queue.dma_start(out=out[:, tokens], in_=result[:])

from contextlib import ExitStack

import concourse.mybir as mybir

D, T, I, Q = 512, 1024, 512, 128
FLOPS = 2 * D * T * Q

F32 = mybir.dt.float32
BF16 = mybir.dt.bfloat16
I32 = mybir.dt.int32
U32 = mybir.dt.uint32
U16 = mybir.dt.uint16
U8 = mybir.dt.uint8
FP8X4 = mybir.dt.float8_e4m3fn_x4
ALU = mybir.AluOpType
ACT = mybir.ActivationFunctionType

P = 128
PACK = 4
QUADRANTS = 4
SCALE_ROWS = 4
HEAD_ROWS = 16
KEY_COLS = T // 2
SLOT_PARTS = 2
PART = I // SLOT_PARTS
SCORE_COLS = (256, 256, 256, 128, 128)
STORE_COLS = 256


def tile_attend_conditioned_lean_putold_heads_kernel(
    tc, query, keys_words, keys_scales, lam, old, offs, offs2, offs3, offs4, out
):
    nc = tc.nc
    with ExitStack() as ctx:
        lists = ctx.enter_context(tc.tile_pool(name="lists", bufs=1))
        sb = ctx.enter_context(tc.tile_pool(name="sb", bufs=1))
        psum = ctx.enter_context(tc.psum_pool(name="psum", bufs=1))

        key_scales = sb.tile([P, T], U8, align_bytes=64)
        nc.vector.memset(key_scales[:].bitcast(I32), 0)

        q_raw = sb.tile([P, PACK, Q], F32, tag="staged")
        nc.sync.dma_start(out=q_raw[:], in_=query.rearrange("(p j) q -> p j q", j=PACK))

        words_hbm = keys_words[0].rearrange("p c r -> p (c r)").bitcast(I32)
        key_words = [
            sb.tile([P, KEY_COLS], I32, name="key_words%d" % u, align_bytes=64) for u in range(T // KEY_COLS)
        ]
        judge = lists.tile([P, I // HEAD_ROWS], U16)
        first = lists.tile([P, I // HEAD_ROWS], U16)
        second = lists.tile([P, I // HEAD_ROWS], U16)
        places = lists.tile([P, I // HEAD_ROWS], U16)

        nc.sync.dma_start(out=key_words[0][:], in_=words_hbm[:, :KEY_COLS])
        for r in range(QUADRANTS):
            queue = nc.scalar if r < QUADRANTS // 2 else nc.sync
            queue.dma_start(
                out=key_scales[32 * r : 32 * r + SCALE_ROWS, :].bitcast(I32),
                in_=keys_scales[0, SCALE_ROWS * r : SCALE_ROWS * (r + 1), :].bitcast(I32),
            )
        nc.sync.dma_start(judge[:], offs2)
        nc.sync.dma_start(out=key_words[1][:], in_=words_hbm[:, KEY_COLS:])
        nc.sync.dma_start(first[:], offs)
        lam_col = sb.tile([P, 1], F32)
        nc.gpsimd.dma_start(out=lam_col[:], in_=lam)
        nc.sync.dma_start(second[:], offs3)
        nc.sync.dma_start(places[:], offs4)
        totals = sb.tile([P, T], F32, tag="staged")
        nc.sync.dma_start(out=totals[:], in_=old)

        placed = sb.tile([P, T], F32)
        nc.vector.memset(placed[:], 0.0)

        warm_in = sb.tile([P, 1], F32)
        warm_out = sb.tile([P, 1], F32)
        nc.vector.memset(warm_in[:], 0.0)
        nc.scalar.activation(warm_out[:], warm_in[:], ACT.Sigmoid)

        q_bf = sb.tile([P, Q, PACK], BF16, align_bytes=64)
        nc.vector.tensor_copy(
            out=q_bf[:].rearrange("p (c i) j -> p c j i", i=4),
            in_=q_raw[:].rearrange("p j (c i) -> p c j i", i=4),
        )
        q_words = sb.tile([P, Q], U32, align_bytes=64)
        q_scales = sb.tile([P, Q], U8, align_bytes=64)
        nc.vector.quantize_mx(
            out=q_words[:].bitcast(FP8X4),
            scales=q_scales[:],
            in_=q_bf[:].rearrange("p q j -> p (q j)"),
        )

        scores = sb.tile([P, T], F32)
        t0 = 0
        for b, n in enumerate(SCORE_COLS):
            bank = psum.tile([P, n], F32, name="bank%d" % b)
            u, lo = divmod(t0, KEY_COLS)
            nc.tensor.matmul_mx(
                out=bank[:],
                lhsT=q_words[:].bitcast(FP8X4),
                lhsT_scale=q_scales[:],
                rhs=key_words[u][:, lo : lo + n].bitcast(FP8X4),
                rhs_scale=key_scales[:, t0 : t0 + n],
                start=True,
                stop=True,
            )
            if b % 2 == 0:
                nc.scalar.copy(scores[:, t0 : t0 + n], bank[:])
            else:
                nc.vector.tensor_copy(scores[:, t0 : t0 + n], bank[:])
            t0 = t0 + n

        neg_lam = sb.tile([P, 1], F32)
        nc.scalar.activation(neg_lam[:], lam_col[:], ACT.Copy, scale=-1.0)

        cols = PART // HEAD_ROWS
        a_first = []
        for h in range(SLOT_PARTS):
            picked = sb.tile([P, PART], F32, name="a_first%d" % h)
            nc.vector.tensor_copy(picked[:], scores[:].indirect(first[:, h * cols : (h + 1) * cols]))
            a_first.append(picked)

        for h in range(SLOT_PARTS):
            entries = slice(h * cols, (h + 1) * cols)
            gate = sb.tile([P, PART], F32, name="gate%d" % h, tag="gate")
            nc.scalar.activation(gate[:], scores[:].indirect(judge[:, entries]), ACT.Sigmoid, scale=2.0)
            neg_second = sb.tile([P, PART], F32, name="neg_second%d" % h)
            nc.scalar.activation(
                neg_second[:], scores[:].indirect(second[:, entries]), ACT.Copy, scale=neg_lam[:]
            )
            term1 = sb.tile([P, PART], F32, name="term1_%d" % h)
            nc.vector.scalar_tensor_tensor(
                term1[:], a_first[h][:], lam_col[:], gate[:], ALU.mult, ALU.mult
            )
            term2 = sb.tile([P, PART], F32, name="term2_%d" % h)
            nc.vector.scalar_tensor_tensor(
                term2[:], gate[:], 1.0, neg_second[:], ALU.subtract, ALU.mult
            )
            nc.vector.tensor_tensor(placed[:].indirect(places[:, entries]), term1[:], term2[:], ALU.add)

        for s in range(T // STORE_COLS):
            tokens = slice(s * STORE_COLS, (s + 1) * STORE_COLS)
            result = sb.tile([P, STORE_COLS], F32, name="result%d" % s)
            nc.vector.tensor_tensor(result[:], placed[:, tokens], totals[:, tokens], ALU.add)
            queue = nc.sync if s % 2 == 0 else nc.scalar
            queue.dma_start(out=out[:, tokens], in_=result[:])
